import numpy as np
import ml_dtypes


def mxq(x, axis, fmt="e4m3"):
    dtype, down = {"e4m3": (ml_dtypes.float8_e4m3fn, 7), "e5m2": (ml_dtypes.float8_e5m2, 14)}[fmt]
    v = np.moveaxis(np.asarray(x, np.float32).astype(ml_dtypes.bfloat16).astype(np.float64), axis, -1)
    blocks = v.reshape(v.shape[:-1] + (-1, 32))
    amax = np.abs(blocks).max(-1, keepdims=True)
    byte = np.maximum(np.where(amax > 0, np.frexp(amax)[1] - 1 + 127, 0) - down, 1)
    scale = np.exp2(byte - 127.0)
    codes = (blocks / scale).astype(np.float32).astype(dtype).astype(np.float64)
    return np.moveaxis((codes * scale).reshape(v.shape), -1, axis)


WIDE = False


def mx_kscale(k):
    if not WIDE:
        return np.ones(k)
    levels = np.array([10, -10, 5, -5, 0])
    if k % 512:
        return np.exp2(np.random.permutation(np.resize(levels, k // 32))).repeat(32)
    a = np.empty((k // 512, 16))
    for p in range(k // 512):
        a[p, :8] = np.random.permutation(np.resize(levels, 8))
        for g in range(8):
            far = levels[np.abs(levels - a[p, g]) >= 10]
            a[p, g + 8] = far[np.random.randint(len(far))]
    return np.exp2(a.ravel()).repeat(32)


def f64(x):
    return np.asarray(x).astype(np.float64)


def striped(idx):
    return np.tile(idx.reshape(-1, 16).T, (8, 1)).astype(np.uint16)


def unstriped(offs):
    return offs[:16].T.reshape(-1).astype(np.int64)


def pack_weight(w):
    k, n = w.shape
    w = f64(np.asarray(w, np.float32).astype(ml_dtypes.bfloat16)).reshape(k // 32, 32, n)
    amax = np.abs(w).max(1)
    byte = np.clip(np.where(amax > 0, np.frexp(amax)[1] - 1 + 127 - 7, 1), 1, 254)
    scaled = (w * np.exp2(127.0 - byte)[:, None, :]).reshape(k, n).astype(np.float32)
    words = np.ascontiguousarray(scaled.reshape(k // 512, 128, 4, n).transpose(0, 1, 3, 2)).astype(ml_dtypes.float8_e4m3fn).view(np.uint8)
    return words, np.ascontiguousarray(byte.astype(np.uint8).reshape(k // 512, 16, n))


def unpack_weight(words, scales):
    g, p, n, _ = words.shape
    vals = np.ascontiguousarray(words).view(ml_dtypes.float8_e4m3fn).astype(np.float64) * np.repeat(np.exp2(scales.astype(np.float64) - 127.0), 8, axis=1)[..., None]
    return vals.transpose(0, 1, 3, 2).reshape(g * 512, n)


def sigmoid(v):
    return 1.0 / (1.0 + np.exp(-np.maximum(v, -700.0)))


K, T, S, D, H, Z, W = 512, 2048, 512, 2, 512, 512, 2048
P = 2 ** 7


def setup_inputs():
    n = np.random.standard_normal
    s = mx_kscale(K)[:, None]
    packed_xT = pack_weight(n((K, T)) * s)
    packed_eT = pack_weight(n((K, W)) * s)
    return {
        "x_words": packed_xT[0],
        "x_scales": packed_xT[1],
        "w1": (n((K, H)) / np.sqrt(K) / s).astype(np.float32),
        "w2": (n((K, H)) / np.sqrt(K) / s).astype(np.float32),
        "e_words": packed_eT[0],
        "e_scales": packed_eT[1],
        "unit": (np.random.uniform(0.6, 1.4, (K, 1)) / np.sqrt(K) / s).astype(np.float32),
        "thr": (np.tile(np.random.uniform(-0.3, 0.6, W), (P, 1))).astype(np.float32),
        "expr": (np.tile(np.random.uniform(0.3, 1.5, W), (P, 1))).astype(np.float32),
        "offs": striped(np.random.permutation(T)[:S]),
        "fl": striped(np.random.permutation(S)),
        "all_": striped(np.random.permutation(W)[:Z]),
    }


def reference(x_words, x_scales, w1, w2, e_words, e_scales, unit, thr, expr, offs, fl, all_):
    xq = unpack_weight(x_words, x_scales)[:, unstriped(offs)]
    y = mxq(f64(w1), 0, "e4m3").T @ xq
    ya = mxq(f64(w2), 0, "e4m3").T @ xq
    af = ya[:, unstriped(fl)]
    ctx = y * (0.8 * sigmoid(af) + 0.4)
    pep = ctx.reshape(len(ctx), -1, D).sum(axis=2)
    absa = np.abs(ya)
    pq = pep + 0.3 * (absa.reshape(len(absa), -1, D).max(axis=2))
    hid = f64(unit) * pq
    e_all_ = unpack_weight(e_words, e_scales)[:, unstriped(all_)]
    sc = mxq(hid, 0, "e4m3").T @ e_all_
    mg = sc - (f64(thr)[:1][:, unstriped(all_)])
    bind = sigmoid(2.5 * mg)
    return bind * (f64(expr)[:1][:, unstriped(all_)])

@@ -1,0 +1,253 @@
+from contextlib import ExitStack
+
+import concourse.mybir as mybir
+from concourse.masks import make_identity
+
+F32 = mybir.dt.float32
+BF16 = mybir.dt.bfloat16
+I32 = mybir.dt.int32
+U32 = mybir.dt.uint32
+U16 = mybir.dt.uint16
+U8 = mybir.dt.uint8
+FP8X4 = mybir.dt.float8_e4m3fn_x4
+ALU = mybir.AluOpType
+ACT = mybir.ActivationFunctionType
+AX = mybir.AxisListType
+
+P = 128
+PACK = 4
+K = 512
+TABLE = 2048
+S = 512
+V = 256
+Z = 512
+HALF = S // 2
+LIST_COLS = S // 16
+
+FLOPS = 2 * K * 512 * S * 2 + 2 * 512 * V * Z
+BYTES = 4 * 1024 * 1024 + 2 * 16 * TABLE + 2 * TABLE * 4 + 512 * 4 + 3 * P * LIST_COLS * 2 + V * Z * 4
+
+
+def tile_picked_yhlaepi_pres_p_kernel(
+    tc, x_words, x_scales, w1, w2, e_words, e_scales, unit, thr, expr, offs, fl, all_, out
+):
+    nc = tc.nc
+    with ExitStack() as ctx:
+        keep = ctx.enter_context(tc.tile_pool(name="keep", bufs=1))
+        psum = ctx.enter_context(tc.psum_pool(name="psum", bufs=1))
+
+        def sb(shape, dtype, name, tag=None):
+            return keep.tile(shape, dtype, name=name, tag=tag or name, align_bytes=64)
+
+        def bank(name, tag):
+            return psum.tile([P, 512], F32, name=name, tag=tag)
+
+        offs_sb = sb([P, LIST_COLS], U16, "offs_sb")
+        all_sb = sb([P, LIST_COLS], U16, "all_sb")
+        fl_sb = sb([P, LIST_COLS], U16, "fl_sb")
+
+        xs_table = sb([P, TABLE], U8, "xs_table", "stage_a")
+        es_table = sb([P, TABLE], U8, "es_table")
+        te_table = sb([P, TABLE], F32, "te_table")
+        nc.vector.memset(xs_table[:].bitcast(I32), 0)
+        nc.vector.memset(es_table[:].bitcast(I32), 0)
+        nc.vector.memset(te_table[:].bitcast(I32), 0)
+
+        def load_weight(w, name, tag):
+            raw = sb([P, PACK, 512], F32, name, tag)
+            nc.sync.dma_start(raw[:], w.rearrange("(p j) c -> p j c", j=PACK))
+            return raw
+
+        def load_words(words, name, tag):
+            table = sb([P, TABLE], I32, name, tag)
+            nc.sync.dma_start(table[:], words[0].rearrange("p c r -> p (c r)").bitcast(I32))
+            return table
+
+        def load_scales(engine, table, scales):
+            for q in range(4):
+                engine.dma_start(
+                    table[32 * q : 32 * q + 4, :].bitcast(I32), scales[0, 4 * q : 4 * q + 4, :].bitcast(I32)
+                )
+
+        nc.sync.dma_start(offs_sb[:], offs)
+        w2_raw = load_weight(w2, "w2_raw", "stage_b")
+        nc.sync.dma_start(all_sb[:], all_)
+        nc.sync.dma_start(fl_sb[:], fl)
+        xw_table = load_words(x_words, "xw_table", "xw_table")
+        load_scales(nc.scalar, xs_table, x_scales)
+        nc.scalar.dma_start(te_table[0:1, :], thr[0:1, :])
+        nc.scalar.dma_start(te_table[1:2, :], expr[0:1, :])
+
+        ident = sb([P, P], F32, "ident")
+        make_identity(nc, ident[:])
+        load_scales(nc.gpsimd, es_table, e_scales)
+        unit_sb = sb([P, PACK], F32, "unit_sb")
+        nc.gpsimd.dma_start(unit_sb[:], unit.rearrange("(p t) o -> p (t o)", t=PACK))
+
+        xs = sb([P, S], U8, "xs")
+        nc.vector.tensor_copy(xs[:], xs_table[:].indirect(offs_sb[:]))
+        w1_raw = load_weight(w1, "w1_raw", "stage_a")
+
+        def quantise_weight(raw, name):
+            codes, scales = [], []
+            src = raw[:].rearrange("p j (m t) -> p m t j", t=PACK)
+            for pair, engine in enumerate((nc.vector, nc.scalar)):
+                grouped = sb([P, 2 * P * PACK], BF16, "%s_grouped%d" % (name, pair))
+                dst = grouped[:].rearrange("p (t m j) -> p m t j", t=2, j=PACK)
+                if pair == 0:
+                    nc.vector.tensor_copy(dst, src[:, :, 0:2, :])
+                else:
+                    nc.scalar.copy(dst, src[:, :, 2:4, :])
+                c = sb([P, 2 * P], U32, "%s_codes%d" % (name, pair))
+                s = sb([P, 2 * P], U8, "%s_scales%d" % (name, pair))
+                nc.vector.quantize_mx(c[:].bitcast(FP8X4), s[:], grouped[:])
+                for i in range(2):
+                    codes.append(c[:, i * P : (i + 1) * P])
+                    scales.append(s[:, i * P : (i + 1) * P])
+            return codes, scales
+
+        w2_codes, w2_scales = quantise_weight(w2_raw, "w2")
+        ew_table = load_words(e_words, "ew_table", "stage_b")
+
+        es = sb([P, Z], U8, "es")
+        nc.vector.tensor_copy(es[:], es_table[:].indirect(all_sb[:]))
+        unit8 = sb([P, PACK], F32, "unit8")
+        nc.vector.tensor_scalar(unit8[:], unit_sb[:], 0.8, None, ALU.mult)
+
+        te = sb([P, Z], F32, "te")
+        nc.scalar.activation(te[:], te_table[:].indirect(all_sb[:]), ACT.Copy)
+        te_turned = bank("te_turned", "bank_s0")
+        for b in range(4):
+            nc.tensor.transpose(te_turned[:, b * P : (b + 1) * P], te[:, b * P : (b + 1) * P], ident[:])
+        te_cols = sb([P, 4, 2], F32, "te_cols")
+        nc.scalar.copy(te_cols[:], te_turned[:].rearrange("p (b r) -> p b r", b=4)[:, :, 0:2])
+        thr_bank = bank("thr_bank", "bank_s1")
+        expr_rows = bank("expr_rows", "bank_expr")
+        for r, target in enumerate((thr_bank, expr_rows)):
+            for b in range(4):
+                nc.tensor.transpose(
+                    target[:, b * P : (b + 1) * P], te_cols[:, b, r : r + 1].to_broadcast([P, P]), ident[:]
+                )
+        thr_rows = sb([P, Z], F32, "thr_rows")
+        nc.scalar.copy(thr_rows[:], thr_bank[:])
+
+        xw = [sb([P, HALF], U32, "xw%d" % h) for h in range(2)]
+        for h in range(2):
+            nc.vector.tensor_copy(xw[h][:], xw_table[:].bitcast(U32).indirect(offs_sb[:, 16 * h : 16 * h + 16]))
+
+        def product(target, codes, scales, h):
+            nc.tensor.matmul_mx(
+                target,
+                lhsT=codes.bitcast(FP8X4),
+                lhsT_scale=scales,
+                rhs=xw[h][:].bitcast(FP8X4),
+                rhs_scale=xs[:, h * HALF : (h + 1) * HALF],
+                start=True,
+                stop=True,
+            )
+
+        ya_banks = [bank("ya_bank%d" % t, "bank%d" % t) for t in range(4)]
+        for pair in range(2):
+            for h in range(2):
+                for t in (2 * pair, 2 * pair + 1):
+                    product(ya_banks[t][:, h * HALF : (h + 1) * HALF], w2_codes[t], w2_scales[t], h)
+
+        ya = [sb([P, S], F32, "ya%d" % t) for t in range(4)]
+        peak = [sb([P, V], F32, "peak%d" % t) for t in range(4)]
+        gate = [[sb([P, 2, HALF], F32, "gate%d_%d" % (h, pair)) for pair in range(2)] for h in range(2)]
+
+        def leave_bank(t):
+            nc.scalar.copy(ya[t][:], ya_banks[t][:])
+
+        def pair_peak(t):
+            nc.vector.tensor_reduce(
+                peak[t][:], ya[t][:].rearrange("p (v d) -> p v d", d=2), AX.X, ALU.max, apply_absolute_value=True
+            )
+
+        def flank_gate(t, h):
+            nc.scalar.activation(
+                gate[h][t // 2][:, t % 2, :], ya[t][:].indirect(fl_sb[:, 16 * h : 16 * h + 16]), ACT.Sigmoid
+            )
+
+        leave_bank(0)
+        w1_codes, w1_scales = quantise_weight(w1_raw, "w1")
+        pair_peak(0)
+        flank_gate(0, 0)
+        for t in range(1, 4):
+            leave_bank(t)
+            pair_peak(t)
+            flank_gate(t, 0)
+
+        ew = sb([P, Z], U32, "ew")
+        nc.vector.tensor_copy(ew[:], ew_table[:].bitcast(U32).indirect(all_sb[:]))
+
+        y_banks = {}
+        for h in range(2):
+            for pair in range(2):
+                y_banks[h, pair] = bank("y_bank%d_%d" % (h, pair), "bank%d" % (2 * h + pair))
+                for i in range(2):
+                    t = 2 * pair + i
+                    product(y_banks[h, pair][:, i * HALF : (i + 1) * HALF], w1_codes[t], w1_scales[t], h)
+
+        def hidden(h):
+            pq = sb([P, PACK, P], F32, "pq%d" % h)
+            for pair in range(2):
+                ctx_pair = sb([P, 2 * HALF], F32, "ctx%d_%d" % (h, pair))
+                nc.vector.scalar_tensor_tensor(
+                    ctx_pair[:],
+                    gate[h][pair][:].rearrange("p i j -> p (i j)"),
+                    0.5,
+                    y_banks[h, pair][:],
+                    ALU.add,
+                    ALU.mult,
+                )
+                members = ctx_pair[:].rearrange("p (i v d) -> p i v d", i=2, d=2)
+                part = sb([P, 2, P], F32, "part%d_%d" % (h, pair))
+                for i in range(2):
+                    nc.vector.scalar_tensor_tensor(
+                        part[:, i, :],
+                        peak[2 * pair + i][:, h * P : (h + 1) * P],
+                        0.375,
+                        members[:, i, :, 0],
+                        ALU.mult,
+                        ALU.add,
+                    )
+                nc.vector.tensor_tensor(pq[:, 2 * pair : 2 * pair + 2, :], part[:], members[:, :, :, 1], ALU.add)
+            hid = sb([P, P, PACK], BF16, "hid%d" % h)
+            nc.vector.tensor_tensor(
+                hid[:],
+                pq[:].rearrange("p t v -> p v t"),
+                unit8[:].unsqueeze(1).to_broadcast([P, P, PACK]),
+                ALU.mult,
+            )
+            codes = sb([P, P], U32, "hid_codes%d" % h)
+            scales = sb([P, P], U8, "hid_scales%d" % h)
+            nc.vector.quantize_mx(codes[:].bitcast(FP8X4), scales[:], hid[:].rearrange("p v t -> p (v t)"))
+            return codes, scales
+
+        def bind(h, codes, scales):
+            for c in range(2):
+                cols = slice(c * HALF, (c + 1) * HALF)
+                score = bank("score%d_%d" % (h, c), "bank_s%d" % c)
+                nc.tensor.matmul_mx(
+                    score[:, 0:HALF],
+                    lhsT=codes[:].bitcast(FP8X4),
+                    lhsT_scale=scales[:],
+                    rhs=ew[:, cols].bitcast(FP8X4),
+                    rhs_scale=es[:, cols],
+                    start=True,
+                    stop=True,
+                )
+                margin = sb([P, HALF], F32, "margin%d_%d" % (h, c))
+                nc.vector.tensor_tensor(margin[:], score[:, 0:HALF], thr_rows[:, cols], ALU.subtract)
+                bound = sb([P, HALF], F32, "bound%d_%d" % (h, c))
+                nc.scalar.activation(bound[:], margin[:], ACT.Sigmoid, scale=2.5)
+                result = sb([P, HALF], F32, "result%d_%d" % (h, c))
+                nc.vector.tensor_tensor(result[:], bound[:], expr_rows[:, cols], ALU.mult)
+                nc.sync.dma_start(out[h * P : (h + 1) * P, cols], result[:])
+
+        first = hidden(0)
+        for t in range(4):
+            flank_gate(t, 1)
+        bind(0, *first)
+        bind(1, *hidden(1))

@@ -12,7 +12,6 @@ U8 = mybir.dt.uint8
 FP8X4 = mybir.dt.float8_e4m3fn_x4
 ALU = mybir.AluOpType
 ACT = mybir.ActivationFunctionType
-AX = mybir.AxisListType
 
 P = 128
 PACK = 4
@@ -23,6 +22,7 @@ V = 256
 Z = 512
 HALF = S // 2
 LIST_COLS = S // 16
+BIG = TABLE * 4
 
 FLOPS = 2 * K * 512 * S * 2 + 2 * 512 * V * Z
 BYTES = 4 * 1024 * 1024 + 2 * 16 * TABLE + 2 * TABLE * 4 + 512 * 4 + 3 * P * LIST_COLS * 2 + V * Z * 4
@@ -34,32 +34,40 @@ def tile_picked_yhlaepi_pres_p_kernel(
     nc = tc.nc
     with ExitStack() as ctx:
         keep = ctx.enter_context(tc.tile_pool(name="keep", bufs=1))
+        stage = ctx.enter_context(tc.tile_pool(name="stage", bufs=1))
         psum = ctx.enter_context(tc.psum_pool(name="psum", bufs=1))
 
-        def sb(shape, dtype, name, tag=None):
-            return keep.tile(shape, dtype, name=name, tag=tag or name, align_bytes=64)
+        def sb(shape, dtype, name):
+            return keep.tile(shape, dtype, name=name, align_bytes=64)
 
-        def bank(name, tag):
-            return psum.tile([P, 512], F32, name=name, tag=tag)
+        def staged(shape, dtype, name, offset, align=32):
+            return stage.tile(shape, dtype, name=name, align_bytes=align, offset=offset)
+
+        def bank(name, number):
+            return psum.tile([P, 512], F32, name=name, tag="bank%d" % number)
 
         offs_sb = sb([P, LIST_COLS], U16, "offs_sb")
         all_sb = sb([P, LIST_COLS], U16, "all_sb")
         fl_sb = sb([P, LIST_COLS], U16, "fl_sb")
 
-        xs_table = sb([P, TABLE], U8, "xs_table", "stage_a")
-        es_table = sb([P, TABLE], U8, "es_table")
-        te_table = sb([P, TABLE], F32, "te_table")
+        xs_table = staged([P, TABLE], U8, "xs_table", 3 * BIG)
+        te_table = staged([P, TABLE], F32, "te_table", 4 * BIG)
+        zeros = staged([P, 16], F32, "zeros", BIG - 32)
+        nc.vector.memset(zeros[:], 0.0)
         nc.vector.memset(xs_table[:].bitcast(I32), 0)
-        nc.vector.memset(es_table[:].bitcast(I32), 0)
-        nc.vector.memset(te_table[:].bitcast(I32), 0)
+        warm_in = sb([P, 1], F32, "warm_in")
+        nc.gpsimd.memset(warm_in[:], 0.0)
+        nc.vector.tensor_copy(
+            te_table[:].rearrange("p (r c) -> p r c", c=16), zeros[:].unsqueeze(1).to_broadcast([P, TABLE // 16, 16])
+        )
 
-        def load_weight(w, name, tag):
-            raw = sb([P, PACK, 512], F32, name, tag)
+        def load_weight(w, name, offset):
+            raw = staged([P, PACK, 512], F32, name, offset)
             nc.sync.dma_start(raw[:], w.rearrange("(p j) c -> p j c", j=PACK))
             return raw
 
-        def load_words(words, name, tag):
-            table = sb([P, TABLE], I32, name, tag)
+        def load_words(words, name, offset):
+            table = staged([P, TABLE], I32, name, offset)
             nc.sync.dma_start(table[:], words[0].rearrange("p c r -> p (c r)").bitcast(I32))
             return table
 
@@ -70,184 +78,214 @@ def tile_picked_yhlaepi_pres_p_kernel(
                 )
 
         nc.sync.dma_start(offs_sb[:], offs)
-        w2_raw = load_weight(w2, "w2_raw", "stage_b")
         nc.sync.dma_start(all_sb[:], all_)
+        w2_raw = load_weight(w2, "w2_raw", 2 * BIG)
         nc.sync.dma_start(fl_sb[:], fl)
-        xw_table = load_words(x_words, "xw_table", "xw_table")
-        load_scales(nc.scalar, xs_table, x_scales)
-        nc.scalar.dma_start(te_table[0:1, :], thr[0:1, :])
-        nc.scalar.dma_start(te_table[1:2, :], expr[0:1, :])
-
-        ident = sb([P, P], F32, "ident")
-        make_identity(nc, ident[:])
-        load_scales(nc.gpsimd, es_table, e_scales)
         unit_sb = sb([P, PACK], F32, "unit_sb")
-        nc.gpsimd.dma_start(unit_sb[:], unit.rearrange("(p t) o -> p (t o)", t=PACK))
+        nc.sync.dma_start(unit_sb[:], unit.rearrange("(p t) o -> p (t o)", t=PACK))
+        load_scales(nc.scalar, xs_table, x_scales)
+        warm = sb([P, 1], F32, "warm")
+        nc.scalar.activation(warm[:], warm_in[:], ACT.Sigmoid)
+        unit8 = sb([P, PACK], F32, "unit8")
+        unit3 = sb([P, PACK], F32, "unit3")
+        nc.gpsimd.tensor_scalar(unit8[:], unit_sb[:], 0.8, 0.0, ALU.mult, ALU.add)
+        nc.gpsimd.tensor_scalar(unit3[:], unit_sb[:], 0.3, 0.0, ALU.mult, ALU.add)
+        xw_table = load_words(x_words, "xw_table", 0)
+        nc.sync.dma_start(te_table[0:1, :], thr[0:1, :])
+        nc.sync.dma_start(te_table[1:2, :], expr[0:1, :])
+        w1_raw = staged([P, 2, PACK, HALF], F32, "w1_raw", BIG)
+        for half in range(2):
+            nc.sync.dma_start(
+                w1_raw[:, half, :, :], w1[:, half * HALF : (half + 1) * HALF].rearrange("(p j) c -> p j c", j=PACK)
+            )
 
         xs = sb([P, S], U8, "xs")
         nc.vector.tensor_copy(xs[:], xs_table[:].indirect(offs_sb[:]))
-        w1_raw = load_weight(w1, "w1_raw", "stage_a")
+        es_table = staged([P, TABLE], U8, "es_table", 3 * BIG)
+        nc.gpsimd.memset(es_table[:].bitcast(I32), 0)
+        load_scales(nc.sync, es_table, e_scales)
 
-        def quantise_weight(raw, name):
-            codes, scales = [], []
-            src = raw[:].rearrange("p j (m t) -> p m t j", t=PACK)
-            for pair, engine in enumerate((nc.vector, nc.scalar)):
-                grouped = sb([P, 2 * P * PACK], BF16, "%s_grouped%d" % (name, pair))
-                dst = grouped[:].rearrange("p (t m j) -> p m t j", t=2, j=PACK)
-                if pair == 0:
-                    nc.vector.tensor_copy(dst, src[:, :, 0:2, :])
-                else:
-                    nc.scalar.copy(dst, src[:, :, 2:4, :])
-                c = sb([P, 2 * P], U32, "%s_codes%d" % (name, pair))
-                s = sb([P, 2 * P], U8, "%s_scales%d" % (name, pair))
-                nc.vector.quantize_mx(c[:].bitcast(FP8X4), s[:], grouped[:])
-                for i in range(2):
-                    codes.append(c[:, i * P : (i + 1) * P])
-                    scales.append(s[:, i * P : (i + 1) * P])
-            return codes, scales
+        w2_codes, w2_scales = [], []
+        w2_view = w2_raw[:].rearrange("p j (m t) -> p m t j", t=PACK)
+        for copy, t0, t1 in ((nc.vector.tensor_copy, 0, 1), (nc.scalar.copy, 1, 4)):
+            n = t1 - t0
+            grouped = staged([P, n * P * PACK], BF16, "w2_grouped%d" % t0, 5 * BIG + t0 * 1024, 64)
+            copy(grouped[:].rearrange("p (t m j) -> p m t j", t=n, j=PACK), w2_view[:, :, t0:t1, :])
+            c = sb([P, n * P], U32, "w2_codes%d" % t0)
+            s = sb([P, n * P], U8, "w2_scales%d" % t0)
+            nc.vector.quantize_mx(c[:].bitcast(FP8X4), s[:], grouped[:])
+            for i in range(n):
+                w2_codes.append(c[:, i * P : (i + 1) * P])
+                w2_scales.append(s[:, i * P : (i + 1) * P])
+        ident = staged([P, P], F32, "ident", 5 * BIG)
+        make_identity(nc, ident[:])
+        ew_table = load_words(e_words, "ew_table", 2 * BIG)
 
-        w2_codes, w2_scales = quantise_weight(w2_raw, "w2")
-        ew_table = load_words(e_words, "ew_table", "stage_b")
-
-        es = sb([P, Z], U8, "es")
-        nc.vector.tensor_copy(es[:], es_table[:].indirect(all_sb[:]))
-        unit8 = sb([P, PACK], F32, "unit8")
-        nc.vector.tensor_scalar(unit8[:], unit_sb[:], 0.8, None, ALU.mult)
-
-        te = sb([P, Z], F32, "te")
-        nc.scalar.activation(te[:], te_table[:].indirect(all_sb[:]), ACT.Copy)
-        te_turned = bank("te_turned", "bank_s0")
-        for b in range(4):
-            nc.tensor.transpose(te_turned[:, b * P : (b + 1) * P], te[:, b * P : (b + 1) * P], ident[:])
-        te_cols = sb([P, 4, 2], F32, "te_cols")
-        nc.scalar.copy(te_cols[:], te_turned[:].rearrange("p (b r) -> p b r", b=4)[:, :, 0:2])
-        thr_bank = bank("thr_bank", "bank_s1")
-        expr_rows = bank("expr_rows", "bank_expr")
-        for r, target in enumerate((thr_bank, expr_rows)):
-            for b in range(4):
-                nc.tensor.transpose(
-                    target[:, b * P : (b + 1) * P], te_cols[:, b, r : r + 1].to_broadcast([P, P]), ident[:]
-                )
-        thr_rows = sb([P, Z], F32, "thr_rows")
-        nc.scalar.copy(thr_rows[:], thr_bank[:])
-
-        xw = [sb([P, HALF], U32, "xw%d" % h) for h in range(2)]
+        xw = staged([P, S], U32, "xw", 5 * BIG + 1024, 64)
         for h in range(2):
-            nc.vector.tensor_copy(xw[h][:], xw_table[:].bitcast(U32).indirect(offs_sb[:, 16 * h : 16 * h + 16]))
+            nc.vector.tensor_copy(
+                xw[:, h * HALF : (h + 1) * HALF],
+                xw_table[:].bitcast(U32).indirect(offs_sb[:, 16 * h : 16 * h + 16]),
+            )
 
-        def product(target, codes, scales, h):
+        def product(target, codes, scales, cols):
             nc.tensor.matmul_mx(
-                target,
+                target[:, cols],
                 lhsT=codes.bitcast(FP8X4),
                 lhsT_scale=scales,
-                rhs=xw[h][:].bitcast(FP8X4),
-                rhs_scale=xs[:, h * HALF : (h + 1) * HALF],
+                rhs=xw[:, cols].bitcast(FP8X4),
+                rhs_scale=xs[:, cols],
                 start=True,
                 stop=True,
             )
 
-        ya_banks = [bank("ya_bank%d" % t, "bank%d" % t) for t in range(4)]
-        for pair in range(2):
-            for h in range(2):
-                for t in (2 * pair, 2 * pair + 1):
-                    product(ya_banks[t][:, h * HALF : (h + 1) * HALF], w2_codes[t], w2_scales[t], h)
+        ya_banks = [bank("ya_bank%d" % t, t) for t in range(4)]
+        for h in range(2):
+            product(ya_banks[0], w2_codes[0], w2_scales[0], slice(h * HALF, (h + 1) * HALF))
+        for t in range(1, 4):
+            product(ya_banks[t], w2_codes[t], w2_scales[t], slice(0, S))
 
-        ya = [sb([P, S], F32, "ya%d" % t) for t in range(4)]
-        peak = [sb([P, V], F32, "peak%d" % t) for t in range(4)]
-        gate = [[sb([P, 2, HALF], F32, "gate%d_%d" % (h, pair)) for pair in range(2)] for h in range(2)]
+        te = staged([P, Z], F32, "te", 6144)
+        nc.vector.tensor_copy(te[:], te_table[:].indirect(all_sb[:]))
+
+        w1_grouped = staged([P, PACK * P * PACK], BF16, "w1_grouped", 0, 64)
+        w1_view = w1_grouped[:].rearrange("p (t m j) -> p m t j", t=PACK, j=PACK)
+        for half in range(2):
+            nc.vector.tensor_copy(
+                w1_view[:, half * 64 : (half + 1) * 64, :, :],
+                w1_raw[:, half, :, :].rearrange("p j (m t) -> p m t j", t=PACK),
+            )
+        w1_codes, w1_scales = [], []
+        for pair in range(2):
+            c = sb([P, 2 * P], U32, "w1_codes%d" % pair)
+            s = sb([P, 2 * P], U8, "w1_scales%d" % pair)
+            nc.vector.quantize_mx(c[:].bitcast(FP8X4), s[:], w1_grouped[:, pair * 1024 : (pair + 1) * 1024])
+            for i in range(2):
+                w1_codes.append(c[:, i * P : (i + 1) * P])
+                w1_scales.append(s[:, i * P : (i + 1) * P])
+
+        y_banks = [bank("y_bank%d" % t, 4 + t) for t in range(4)]
+        for t in range(4):
+            product(y_banks[t], w1_codes[t], w1_scales[t], slice(0, S))
+
+        sig_size = []
+        gate = [staged([P, S], F32, "gate%d" % t, 6 * BIG + 2048 * t) for t in range(3)]
+        peak_at = [0, 1024, 2048, 6 * BIG + 4096]
+        peak = []
+        part = sb([P, PACK, V], F32, "part")
 
         def leave_bank(t):
-            nc.scalar.copy(ya[t][:], ya_banks[t][:])
+            sig_size.append(staged([P, 2 * S], F32, "sig_size%d" % t, 7 * BIG + 4096 * (t % 3)))
+            nc.scalar.activation(sig_size[t][:, 0:S], ya_banks[t][:], ACT.Sigmoid)
+            nc.scalar.activation(sig_size[t][:, S : 2 * S], ya_banks[t][:], ACT.Abs)
 
         def pair_peak(t):
-            nc.vector.tensor_reduce(
-                peak[t][:], ya[t][:].rearrange("p (v d) -> p v d", d=2), AX.X, ALU.max, apply_absolute_value=True
-            )
+            peak.append(staged([P, V], F32, "peak%d" % t, peak_at[t]))
+            pairs = sig_size[t][:, S : 2 * S].rearrange("p (v d) -> p d v", d=2)
+            nc.vector.tensor_tensor(peak[t][:], pairs[:, 0, :], pairs[:, 1, :], ALU.max)
 
-        def flank_gate(t, h):
+        def gated(t, v0, v1):
+            cols = slice(2 * v0, 2 * v1)
             nc.scalar.activation(
-                gate[h][t // 2][:, t % 2, :], ya[t][:].indirect(fl_sb[:, 16 * h : 16 * h + 16]), ACT.Sigmoid
+                gate[t][:, cols], sig_size[t][:].indirect(fl_sb[:, v0 // 8 : v1 // 8]), ACT.Copy, bias=0.5
+            )
+            nc.vector.scalar_tensor_tensor(
+                members[:, t, :, v0:v1].rearrange("p d v -> p v d"),
+                y_banks[t][:, cols].rearrange("p (v d) -> p v d", d=2),
+                unit8[:, t : t + 1],
+                gate[t][:, cols].rearrange("p (v d) -> p v d", d=2),
+                ALU.mult,
+                ALU.mult,
+            )
+            nc.vector.scalar_tensor_tensor(
+                part[:, t, v0:v1], peak[t][:, v0:v1], unit3[:, t : t + 1], members[:, t, 0, v0:v1], ALU.mult, ALU.add
             )
 
-        leave_bank(0)
-        w1_codes, w1_scales = quantise_weight(w1_raw, "w1")
-        pair_peak(0)
-        flank_gate(0, 0)
-        for t in range(1, 4):
-            leave_bank(t)
-            pair_peak(t)
-            flank_gate(t, 0)
-
-        ew = sb([P, Z], U32, "ew")
-        nc.vector.tensor_copy(ew[:], ew_table[:].bitcast(U32).indirect(all_sb[:]))
-
-        y_banks = {}
-        for h in range(2):
-            for pair in range(2):
-                y_banks[h, pair] = bank("y_bank%d_%d" % (h, pair), "bank%d" % (2 * h + pair))
-                for i in range(2):
-                    t = 2 * pair + i
-                    product(y_banks[h, pair][:, i * HALF : (i + 1) * HALF], w1_codes[t], w1_scales[t], h)
-
-        def hidden(h):
-            pq = sb([P, PACK, P], F32, "pq%d" % h)
-            for pair in range(2):
-                ctx_pair = sb([P, 2 * HALF], F32, "ctx%d_%d" % (h, pair))
-                nc.vector.scalar_tensor_tensor(
-                    ctx_pair[:],
-                    gate[h][pair][:].rearrange("p i j -> p (i j)"),
-                    0.5,
-                    y_banks[h, pair][:],
-                    ALU.add,
-                    ALU.mult,
-                )
-                members = ctx_pair[:].rearrange("p (i v d) -> p i v d", i=2, d=2)
-                part = sb([P, 2, P], F32, "part%d_%d" % (h, pair))
-                for i in range(2):
-                    nc.vector.scalar_tensor_tensor(
-                        part[:, i, :],
-                        peak[2 * pair + i][:, h * P : (h + 1) * P],
-                        0.375,
-                        members[:, i, :, 0],
-                        ALU.mult,
-                        ALU.add,
-                    )
-                nc.vector.tensor_tensor(pq[:, 2 * pair : 2 * pair + 2, :], part[:], members[:, :, :, 1], ALU.add)
-            hid = sb([P, P, PACK], BF16, "hid%d" % h)
+        def quantise_hidden(h):
+            hid = sb([P, P * PACK], BF16, "hid%d" % h)
             nc.vector.tensor_tensor(
-                hid[:],
-                pq[:].rearrange("p t v -> p v t"),
-                unit8[:].unsqueeze(1).to_broadcast([P, P, PACK]),
-                ALU.mult,
+                hid[:].rearrange("p (c i t) -> p c t i", i=4, t=PACK),
+                part[:, :, h * P : (h + 1) * P].rearrange("p t (c i) -> p c t i", i=4),
+                members[:, :, 1, h * P : (h + 1) * P].rearrange("p t (c i) -> p c t i", i=4),
+                ALU.add,
             )
             codes = sb([P, P], U32, "hid_codes%d" % h)
             scales = sb([P, P], U8, "hid_scales%d" % h)
-            nc.vector.quantize_mx(codes[:].bitcast(FP8X4), scales[:], hid[:].rearrange("p v t -> p (v t)"))
+            nc.vector.quantize_mx(codes[:].bitcast(FP8X4), scales[:], hid[:])
             return codes, scales
 
-        def bind(h, codes, scales):
-            for c in range(2):
-                cols = slice(c * HALF, (c + 1) * HALF)
-                score = bank("score%d_%d" % (h, c), "bank_s%d" % c)
+        for t in range(3):
+            leave_bank(t)
+        pair_peak(0)
+        ew = staged([P, Z], U32, "ew", 3072, 64)
+        nc.vector.tensor_copy(ew[:], ew_table[:].bitcast(U32).indirect(all_sb[:]))
+        es = staged([P, Z], U8, "es", BIG, 64)
+        nc.vector.tensor_copy(es[:], es_table[:].indirect(all_sb[:]))
+        pair_peak(1)
+        pair_peak(2)
+        members = staged([P, PACK, 2, V], F32, "members", 2 * BIG + 4096)
+        gated(0, 0, V)
+        gated(1, 0, V)
+        gated(2, 0, V)
+        leave_bank(3)
+        pair_peak(3)
+
+        te_turned = bank("te_turned", 4)
+        for b in range(4):
+            nc.tensor.transpose(te_turned[:, b * P : (b + 1) * P], te[:, b * P : (b + 1) * P], ident[:])
+
+        def score(h, codes, scales):
+            scores = [bank("score%d_%d" % (h, c), ((0, 1), (2, 3))[h][c]) for c in range(2)]
+            for b in range(4):
                 nc.tensor.matmul_mx(
-                    score[:, 0:HALF],
-                    lhsT=codes[:].bitcast(FP8X4),
-                    lhsT_scale=scales[:],
-                    rhs=ew[:, cols].bitcast(FP8X4),
-                    rhs_scale=es[:, cols],
+                    scores[b // 2][:, (b % 2) * P : (b % 2 + 1) * P],
+                    lhsT=ew[:, b * P : (b + 1) * P].bitcast(FP8X4),
+                    lhsT_scale=es[:, b * P : (b + 1) * P],
+                    rhs=codes[:].bitcast(FP8X4),
+                    rhs_scale=scales[:],
                     start=True,
                     stop=True,
                 )
-                margin = sb([P, HALF], F32, "margin%d_%d" % (h, c))
-                nc.vector.tensor_tensor(margin[:], score[:, 0:HALF], thr_rows[:, cols], ALU.subtract)
-                bound = sb([P, HALF], F32, "bound%d_%d" % (h, c))
-                nc.scalar.activation(bound[:], margin[:], ACT.Sigmoid, scale=2.5)
-                result = sb([P, HALF], F32, "result%d_%d" % (h, c))
-                nc.vector.tensor_tensor(result[:], bound[:], expr_rows[:, cols], ALU.mult)
-                nc.sync.dma_start(out[h * P : (h + 1) * P, cols], result[:])
+            return scores
 
-        first = hidden(0)
-        for t in range(4):
-            flank_gate(t, 1)
-        bind(0, *first)
-        bind(1, *hidden(1))
+        def bind(h, c, scores):
+            cols = slice(c * HALF, (c + 1) * HALF)
+            turned = bank("turned%d_%d" % (h, c), ((6, 4), (7, 0))[h][c])
+            for i in range(2):
+                b = 2 * c + i
+                bound = sb([P, P], F32, "bound%d_%d" % (h, b))
+                nc.scalar.activation(
+                    bound[:],
+                    scores[c][:, i * P : (i + 1) * P],
+                    ACT.Sigmoid,
+                    bias=thr_bias[:, b : b + 1],
+                    scale=2.5,
+                )
+                nc.tensor.transpose(turned[:, i * P : (i + 1) * P], bound[:], ident[:])
+            result = sb([P, HALF], F32, "result%d_%d" % (h, c))
+            nc.vector.tensor_tensor(result[:], turned[:, 0:HALF], expr_rows[:, cols], ALU.mult)
+            nc.sync.dma_start(out[h * P : (h + 1) * P, cols], result[:])
+
+        gate.append(staged([P, S], F32, "gate3", 0))
+        gated(3, 0, P)
+        first = quantise_hidden(0)
+        gated(3, P, V)
+        te_view = te_turned[:].rearrange("p (b r) -> p r b", b=4)
+        thr_bias = staged([P, 4], F32, "thr_bias", 7 * BIG)
+        expr_cols = staged([P, 4], F32, "expr_cols", 7 * BIG + 32)
+        nc.scalar.copy(expr_cols[:], te_view[:, 1, :])
+        nc.scalar.activation(thr_bias[:], te_view[:, 0, :], ACT.Copy, scale=-2.5)
+        expr_bank = bank("expr_bank", 5)
+        for b in range(4):
+            nc.tensor.transpose(
+                expr_bank[:, b * P : (b + 1) * P], expr_cols[:, b : b + 1].to_broadcast([P, P]), ident[:]
+            )
+        expr_rows = sb([P, Z], F32, "expr_rows")
+        nc.scalar.copy(expr_rows[:], expr_bank[:])
+        second = quantise_hidden(1)
+        scores0 = score(0, *first)
+        scores1 = score(1, *second)
+        for c in range(2):
+            bind(0, c, scores0)
+        for c in range(2):
+            bind(1, c, scores1)

@@ -121,6 +121,9 @@ def tile_picked_yhlaepi_pres_p_kernel(
         make_identity(nc, ident[:])
         ew_table = load_words(e_words, "ew_table", 2 * BIG)
 
+        te = sb([P, Z], F32, "te")
+        nc.scalar.activation(te[:], te_table[:].indirect(all_sb[:]), ACT.Copy)
+
         xw = staged([P, S], U32, "xw", 5 * BIG + 1024, 64)
         for h in range(2):
             nc.vector.tensor_copy(
@@ -139,14 +142,11 @@ def tile_picked_yhlaepi_pres_p_kernel(
                 stop=True,
             )
 
-        ya_banks = [bank("ya_bank%d" % t, t) for t in range(4)]
-        for h in range(2):
-            product(ya_banks[0], w2_codes[0], w2_scales[0], slice(h * HALF, (h + 1) * HALF))
-        for t in range(1, 4):
-            product(ya_banks[t], w2_codes[t], w2_scales[t], slice(0, S))
-
-        te = staged([P, Z], F32, "te", 6144)
-        nc.vector.tensor_copy(te[:], te_table[:].indirect(all_sb[:]))
+        ya_pieces = [[(bank("ya_bank0_%d" % h, 7 * h), slice(h * HALF, (h + 1) * HALF)) for h in range(2)]]
+        ya_pieces.extend([(bank("ya_bank%d" % t, t), slice(0, S))] for t in range(1, 4))
+        for t in range(4):
+            for target, cols in ya_pieces[t]:
+                product(target, w2_codes[t], w2_scales[t], cols)
 
         w1_grouped = staged([P, PACK * P * PACK], BF16, "w1_grouped", 0, 64)
         w1_view = w1_grouped[:].rearrange("p (t m j) -> p m t j", t=PACK, j=PACK)
@@ -176,8 +176,9 @@ def tile_picked_yhlaepi_pres_p_kernel(
 
         def leave_bank(t):
             sig_size.append(staged([P, 2 * S], F32, "sig_size%d" % t, 7 * BIG + 4096 * (t % 3)))
-            nc.scalar.activation(sig_size[t][:, 0:S], ya_banks[t][:], ACT.Sigmoid)
-            nc.scalar.activation(sig_size[t][:, S : 2 * S], ya_banks[t][:], ACT.Abs)
+            for source, cols in ya_pieces[t]:
+                nc.scalar.activation(sig_size[t][:, 0:S][:, cols], source[:, cols], ACT.Sigmoid)
+                nc.scalar.activation(sig_size[t][:, S : 2 * S][:, cols], source[:, cols], ACT.Abs)
 
         def pair_peak(t):
             peak.append(staged([P, V], F32, "peak%d" % t, peak_at[t]))

from contextlib import ExitStack

import concourse.mybir as mybir
from concourse.masks import make_identity

F32 = mybir.dt.float32
BF16 = mybir.dt.bfloat16
I32 = mybir.dt.int32
U32 = mybir.dt.uint32
U16 = mybir.dt.uint16
U8 = mybir.dt.uint8
FP8X4 = mybir.dt.float8_e4m3fn_x4
ALU = mybir.AluOpType
ACT = mybir.ActivationFunctionType

P = 128
PACK = 4
K = 512
TABLE = 2048
S = 512
V = 256
Z = 512
HALF = S // 2
LIST_COLS = S // 16
BIG = TABLE * 4

FLOPS = 2 * K * 512 * S * 2 + 2 * 512 * V * Z
BYTES = 4 * 1024 * 1024 + 2 * 16 * TABLE + 2 * TABLE * 4 + 512 * 4 + 3 * P * LIST_COLS * 2 + V * Z * 4


def tile_picked_yhlaepi_pres_p_kernel(
    tc, x_words, x_scales, w1, w2, e_words, e_scales, unit, thr, expr, offs, fl, all_, out
):
    nc = tc.nc
    with ExitStack() as ctx:
        keep = ctx.enter_context(tc.tile_pool(name="keep", bufs=1))
        stage = ctx.enter_context(tc.tile_pool(name="stage", bufs=1))
        psum = ctx.enter_context(tc.psum_pool(name="psum", bufs=1))

        def sb(shape, dtype, name):
            return keep.tile(shape, dtype, name=name, align_bytes=64)

        def staged(shape, dtype, name, offset, align=32):
            return stage.tile(shape, dtype, name=name, align_bytes=align, offset=offset)

        def bank(name, number):
            return psum.tile([P, 512], F32, name=name, tag="bank%d" % number)

        offs_sb = sb([P, LIST_COLS], U16, "offs_sb")
        all_sb = sb([P, LIST_COLS], U16, "all_sb")
        fl_sb = sb([P, LIST_COLS], U16, "fl_sb")

        xs_table = staged([P, TABLE], U8, "xs_table", 3 * BIG)
        te_table = staged([P, TABLE], F32, "te_table", 4 * BIG)
        zeros = staged([P, 16], F32, "zeros", BIG - 32)
        nc.vector.memset(zeros[:], 0.0)
        nc.vector.memset(xs_table[:].bitcast(I32), 0)
        warm_in = sb([P, 1], F32, "warm_in")
        nc.gpsimd.memset(warm_in[:], 0.0)
        nc.vector.tensor_copy(
            te_table[:].rearrange("p (r c) -> p r c", c=16), zeros[:].unsqueeze(1).to_broadcast([P, TABLE // 16, 16])
        )

        def load_weight(w, name, offset):
            raw = staged([P, PACK, 512], F32, name, offset)
            nc.sync.dma_start(raw[:], w.rearrange("(p j) c -> p j c", j=PACK))
            return raw

        def load_words(words, name, offset):
            table = staged([P, TABLE], I32, name, offset)
            nc.sync.dma_start(table[:], words[0].rearrange("p c r -> p (c r)").bitcast(I32))
            return table

        def load_scales(engine, table, scales):
            for q in range(4):
                engine.dma_start(
                    table[32 * q : 32 * q + 4, :].bitcast(I32), scales[0, 4 * q : 4 * q + 4, :].bitcast(I32)
                )

        nc.sync.dma_start(offs_sb[:], offs)
        nc.sync.dma_start(all_sb[:], all_)
        w2_raw = load_weight(w2, "w2_raw", 2 * BIG)
        nc.sync.dma_start(fl_sb[:], fl)
        unit_sb = sb([P, PACK], F32, "unit_sb")
        nc.sync.dma_start(unit_sb[:], unit.rearrange("(p t) o -> p (t o)", t=PACK))
        load_scales(nc.scalar, xs_table, x_scales)
        warm = sb([P, 1], F32, "warm")
        nc.scalar.activation(warm[:], warm_in[:], ACT.Sigmoid)
        unit8 = sb([P, PACK], F32, "unit8")
        unit3 = sb([P, PACK], F32, "unit3")
        nc.gpsimd.tensor_scalar(unit8[:], unit_sb[:], 0.8, 0.0, ALU.mult, ALU.add)
        nc.gpsimd.tensor_scalar(unit3[:], unit_sb[:], 0.3, 0.0, ALU.mult, ALU.add)
        xw_table = load_words(x_words, "xw_table", 0)
        nc.sync.dma_start(te_table[0:1, :], thr[0:1, :])
        nc.sync.dma_start(te_table[1:2, :], expr[0:1, :])
        w1_raw = staged([P, 2, PACK, HALF], F32, "w1_raw", BIG)
        for half in range(2):
            nc.sync.dma_start(
                w1_raw[:, half, :, :], w1[:, half * HALF : (half + 1) * HALF].rearrange("(p j) c -> p j c", j=PACK)
            )

        xs = sb([P, S], U8, "xs")
        nc.vector.tensor_copy(xs[:], xs_table[:].indirect(offs_sb[:]))
        es_table = staged([P, TABLE], U8, "es_table", 3 * BIG)
        nc.gpsimd.memset(es_table[:].bitcast(I32), 0)
        load_scales(nc.sync, es_table, e_scales)

        w2_codes, w2_scales = [], []
        w2_view = w2_raw[:].rearrange("p j (m t) -> p m t j", t=PACK)
        for copy, t0, t1 in ((nc.vector.tensor_copy, 0, 1), (nc.scalar.copy, 1, 4)):
            n = t1 - t0
            grouped = staged([P, n * P * PACK], BF16, "w2_grouped%d" % t0, 5 * BIG + t0 * 1024, 64)
            copy(grouped[:].rearrange("p (t m j) -> p m t j", t=n, j=PACK), w2_view[:, :, t0:t1, :])
            c = sb([P, n * P], U32, "w2_codes%d" % t0)
            s = sb([P, n * P], U8, "w2_scales%d" % t0)
            nc.vector.quantize_mx(c[:].bitcast(FP8X4), s[:], grouped[:])
            for i in range(n):
                w2_codes.append(c[:, i * P : (i + 1) * P])
                w2_scales.append(s[:, i * P : (i + 1) * P])
        ident = staged([P, P], F32, "ident", 5 * BIG)
        make_identity(nc, ident[:])
        ew_table = load_words(e_words, "ew_table", 2 * BIG)

        te = sb([P, Z], F32, "te")
        nc.scalar.activation(te[:], te_table[:].indirect(all_sb[:]), ACT.Copy)

        xw = staged([P, S], U32, "xw", 5 * BIG + 1024, 64)
        for h in range(2):
            nc.vector.tensor_copy(
                xw[:, h * HALF : (h + 1) * HALF],
                xw_table[:].bitcast(U32).indirect(offs_sb[:, 16 * h : 16 * h + 16]),
            )

        def product(target, codes, scales, cols):
            nc.tensor.matmul_mx(
                target[:, cols],
                lhsT=codes.bitcast(FP8X4),
                lhsT_scale=scales,
                rhs=xw[:, cols].bitcast(FP8X4),
                rhs_scale=xs[:, cols],
                start=True,
                stop=True,
            )

        ya_pieces = [[(bank("ya_bank0_%d" % h, 7 * h), slice(h * HALF, (h + 1) * HALF)) for h in range(2)]]
        ya_pieces.extend([(bank("ya_bank%d" % t, t), slice(0, S))] for t in range(1, 4))
        for t in range(4):
            for target, cols in ya_pieces[t]:
                product(target, w2_codes[t], w2_scales[t], cols)

        w1_grouped = staged([P, PACK * P * PACK], BF16, "w1_grouped", 0, 64)
        w1_view = w1_grouped[:].rearrange("p (t m j) -> p m t j", t=PACK, j=PACK)
        for half in range(2):
            nc.vector.tensor_copy(
                w1_view[:, half * 64 : (half + 1) * 64, :, :],
                w1_raw[:, half, :, :].rearrange("p j (m t) -> p m t j", t=PACK),
            )
        w1_codes, w1_scales = [], []
        for pair in range(2):
            c = sb([P, 2 * P], U32, "w1_codes%d" % pair)
            s = sb([P, 2 * P], U8, "w1_scales%d" % pair)
            nc.vector.quantize_mx(c[:].bitcast(FP8X4), s[:], w1_grouped[:, pair * 1024 : (pair + 1) * 1024])
            for i in range(2):
                w1_codes.append(c[:, i * P : (i + 1) * P])
                w1_scales.append(s[:, i * P : (i + 1) * P])

        y_banks = [bank("y_bank%d" % t, 4 + t) for t in range(4)]
        for t in range(4):
            product(y_banks[t], w1_codes[t], w1_scales[t], slice(0, S))

        sig_size = []
        gate = [staged([P, S], F32, "gate%d" % t, 6 * BIG + 2048 * t) for t in range(3)]
        peak_at = [0, 1024, 2048, 6 * BIG + 4096]
        peak = []
        part = sb([P, PACK, V], F32, "part")

        def leave_bank(t):
            sig_size.append(staged([P, 2 * S], F32, "sig_size%d" % t, 7 * BIG + 4096 * (t % 3)))
            for source, cols in ya_pieces[t]:
                nc.scalar.activation(sig_size[t][:, 0:S][:, cols], source[:, cols], ACT.Sigmoid)
                nc.scalar.activation(sig_size[t][:, S : 2 * S][:, cols], source[:, cols], ACT.Abs)

        def pair_peak(t):
            peak.append(staged([P, V], F32, "peak%d" % t, peak_at[t]))
            pairs = sig_size[t][:, S : 2 * S].rearrange("p (v d) -> p d v", d=2)
            nc.vector.tensor_tensor(peak[t][:], pairs[:, 0, :], pairs[:, 1, :], ALU.max)

        def gated(t, v0, v1):
            cols = slice(2 * v0, 2 * v1)
            nc.scalar.activation(
                gate[t][:, cols], sig_size[t][:].indirect(fl_sb[:, v0 // 8 : v1 // 8]), ACT.Copy, bias=0.5
            )
            nc.vector.scalar_tensor_tensor(
                members[:, t, :, v0:v1].rearrange("p d v -> p v d"),
                y_banks[t][:, cols].rearrange("p (v d) -> p v d", d=2),
                unit8[:, t : t + 1],
                gate[t][:, cols].rearrange("p (v d) -> p v d", d=2),
                ALU.mult,
                ALU.mult,
            )
            nc.vector.scalar_tensor_tensor(
                part[:, t, v0:v1], peak[t][:, v0:v1], unit3[:, t : t + 1], members[:, t, 0, v0:v1], ALU.mult, ALU.add
            )

        def quantise_hidden(h):
            hid = sb([P, P * PACK], BF16, "hid%d" % h)
            nc.vector.tensor_tensor(
                hid[:].rearrange("p (c i t) -> p c t i", i=4, t=PACK),
                part[:, :, h * P : (h + 1) * P].rearrange("p t (c i) -> p c t i", i=4),
                members[:, :, 1, h * P : (h + 1) * P].rearrange("p t (c i) -> p c t i", i=4),
                ALU.add,
            )
            codes = sb([P, P], U32, "hid_codes%d" % h)
            scales = sb([P, P], U8, "hid_scales%d" % h)
            nc.vector.quantize_mx(codes[:].bitcast(FP8X4), scales[:], hid[:])
            return codes, scales

        for t in range(3):
            leave_bank(t)
        pair_peak(0)
        ew = staged([P, Z], U32, "ew", 3072, 64)
        nc.vector.tensor_copy(ew[:], ew_table[:].bitcast(U32).indirect(all_sb[:]))
        es = staged([P, Z], U8, "es", BIG, 64)
        nc.vector.tensor_copy(es[:], es_table[:].indirect(all_sb[:]))
        pair_peak(1)
        pair_peak(2)
        members = staged([P, PACK, 2, V], F32, "members", 2 * BIG + 4096)
        gated(0, 0, V)
        gated(1, 0, V)
        gated(2, 0, V)
        leave_bank(3)
        pair_peak(3)

        te_turned = bank("te_turned", 4)
        for b in range(4):
            nc.tensor.transpose(te_turned[:, b * P : (b + 1) * P], te[:, b * P : (b + 1) * P], ident[:])

        def score(h, codes, scales):
            scores = [bank("score%d_%d" % (h, c), ((0, 1), (2, 3))[h][c]) for c in range(2)]
            for b in range(4):
                nc.tensor.matmul_mx(
                    scores[b // 2][:, (b % 2) * P : (b % 2 + 1) * P],
                    lhsT=ew[:, b * P : (b + 1) * P].bitcast(FP8X4),
                    lhsT_scale=es[:, b * P : (b + 1) * P],
                    rhs=codes[:].bitcast(FP8X4),
                    rhs_scale=scales[:],
                    start=True,
                    stop=True,
                )
            return scores

        def bind(h, c, scores):
            cols = slice(c * HALF, (c + 1) * HALF)
            turned = bank("turned%d_%d" % (h, c), ((6, 4), (7, 0))[h][c])
            for i in range(2):
                b = 2 * c + i
                bound = sb([P, P], F32, "bound%d_%d" % (h, b))
                nc.scalar.activation(
                    bound[:],
                    scores[c][:, i * P : (i + 1) * P],
                    ACT.Sigmoid,
                    bias=thr_bias[:, b : b + 1],
                    scale=2.5,
                )
                nc.tensor.transpose(turned[:, i * P : (i + 1) * P], bound[:], ident[:])
            result = sb([P, HALF], F32, "result%d_%d" % (h, c))
            nc.vector.tensor_tensor(result[:], turned[:, 0:HALF], expr_rows[:, cols], ALU.mult)
            nc.sync.dma_start(out[h * P : (h + 1) * P, cols], result[:])

        gate.append(staged([P, S], F32, "gate3", 0))
        gated(3, 0, P)
        first = quantise_hidden(0)
        gated(3, P, V)
        te_view = te_turned[:].rearrange("p (b r) -> p r b", b=4)
        thr_bias = staged([P, 4], F32, "thr_bias", 7 * BIG)
        expr_cols = staged([P, 4], F32, "expr_cols", 7 * BIG + 32)
        nc.scalar.copy(expr_cols[:], te_view[:, 1, :])
        nc.scalar.activation(thr_bias[:], te_view[:, 0, :], ACT.Copy, scale=-2.5)
        expr_bank = bank("expr_bank", 5)
        for b in range(4):
            nc.tensor.transpose(
                expr_bank[:, b * P : (b + 1) * P], expr_cols[:, b : b + 1].to_broadcast([P, P]), ident[:]
            )
        expr_rows = sb([P, Z], F32, "expr_rows")
        nc.scalar.copy(expr_rows[:], expr_bank[:])
        second = quantise_hidden(1)
        scores0 = score(0, *first)
        scores1 = score(1, *second)
        for c in range(2):
            bind(0, c, scores0)
        for c in range(2):
            bind(1, c, scores1)
